import numpy as np, ml_dtypes
CORES = [24,25,26,27,28,29,30,31]
N = 8
BF = ml_dtypes.bfloat16
def gentries(a):
    return np.ascontiguousarray(a.reshape(8, 16, -1).transpose(0, 2, 1)).reshape(8, -1)
def gtable(e):
    e = np.asarray(e); return np.ascontiguousarray(e.reshape(8, -1, 16).transpose(0, 2, 1)).reshape(128, -1).astype(np.int32)
V, L, C, RO, MIN, SH = 512, 16, 4, 2, 7, 4
T = N * V; LN = L // N; H = T // C
def lists(rng):
    return np.argsort(rng.random((8, L, T)), axis=-1).reshape(8, L, C, H)
def turn(pm):
    hl = np.zeros((8, L, T), np.int64)
    np.put_along_axis(hl, pm.reshape(8, L, T), np.broadcast_to(np.tile(np.arange(H), C), (8, L, T)), 2)
    return hl
def parts(rng):
    s = rng.permutation(np.array([24, 48, 64, 96, 128, 160, 200, 256])); lo = rng.integers(0, (257 - s)[:, None], (8, 16))
    x = lo[:, :, None] + rng.integers(0, s[:, None, None], (8, 16, T))
    hits = lo[:, :, None, None] + rng.integers(0, s[:, None, None, None], (8, 16, L, H))
    th = (6 * s[:, None] * rng.random((8, T)) ** 2).astype(np.int64)
    return x, hits, lists(rng), th
def pack(x, hits, pm, th):
    hl = turn(pm).reshape(8, L, N, V).transpose(2, 0, 1, 3).reshape(N, 8, L * V)
    cl = pm.reshape(8, N, LN, C, H).transpose(1, 0, 3, 2, 4).reshape(N, 8, C * LN * H)
    return {"fx": np.ascontiguousarray(x.reshape(8, 16, N, V).transpose(2, 0, 1, 3)).reshape(N, 128, V).astype(np.float32).astype(BF),
            "hv": np.ascontiguousarray(hits.reshape(8, 16, N, LN * H).transpose(2, 0, 1, 3)).reshape(N, 128, LN * H).astype(np.float32).astype(BF),
            "hl": np.stack([gtable(a) for a in hl]), "cl": np.stack([gtable(a) for a in cl]),
            "th": np.ascontiguousarray(th.reshape(8, N, V).transpose(1, 0, 2)).astype(np.int32)}
def contest(x, hits, live, pm):
    out = []
    for l in range(L):
        best = np.full((8, H), 2 ** 24, np.int64)
        for c in range(C):
            t = pm[:, l, c]
            d = np.add.reduce(np.abs(hits[:, :, l] - np.take_along_axis(x, t[:, None, :], 2)), axis=1)
            best = np.minimum(best, np.where(np.take_along_axis(live[:, l], t, 1), d * 4096 + t, 2 ** 24))
        out.append(best & 4095)
    return np.stack(out, axis=1)
def apart(x, b, hl):
    who = np.stack([np.take_along_axis(b[:, l], hl[:, l], 1) for l in range(L)], axis=1)
    e = np.stack([np.add.reduce(np.abs(x - np.take_along_axis(x, who[:, l][:, None, :], 2)), axis=1) for l in range(L)], axis=1)
    return who, e
def classes(rng):
    p = C * np.argsort(rng.random((L, C, H)), axis=2) + np.arange(C)[None, :, None]
    return np.take_along_axis(p, np.argsort(rng.random((L, C, H)), axis=1), axis=1)
def far(rng):
    c = np.arange(T) % C; x = rng.integers(1, 129, (16, T)); x[:, c == 0] = 0
    top = 255 - (rng.random((16, T)) < rng.choice(np.array([0.0, 0.1, 0.3]), T)).astype(np.int64)
    hits = np.full((16, L, H), 255); hits[:, rng.integers(0, L)] = 0
    th = np.where(c == 1, np.add.reduce(top, axis=0) + rng.integers(0, 2, T), 4081)
    return np.where(c == 1, top, x), hits, classes(rng), th
def fall(rng):
    x = 50 * (np.arange(T) % C) + rng.integers(0, 16, (16, T))
    hits = 50 * (np.arange(L) % C)[None, :, None] + rng.integers(0, 16, (16, L, H))
    return x, hits, classes(rng)
def late(rng):
    c = np.arange(T) % C
    x = rng.integers(0, 4, (16, T)) + np.where(c == 0, 0, np.where(c == 1, 208, np.where(c == 2, 200, 100)))
    hits = rng.integers(0, 4, (16, L, H))
    if RO > 2: hits[:, rng.integers(0, L)] += 200
    th = np.where(c == 0, 4081, np.where(c == 1, rng.integers(177, 369, T), 0))
    return x, hits, classes(rng), th
def setup_inputs(rng):
    return pack(*parts(rng))
def setup_inputs_ties(rng):
    x, hits, pm, th = parts(rng); lo = rng.integers(0, 253, (8, 16))
    x = lo[:, :, None] + rng.integers(0, 3, (8, 16, T)); hits = lo[:, :, None, None] + rng.integers(0, 3, (8, 16, L, H))
    for g in (2, 5): x[g] = x[g][:, rng.integers(0, 8, T)]
    e = apart(x, contest(x, hits, np.ones((8, L, T), bool), pm), turn(pm))[1]
    at = np.take_along_axis(e, rng.integers(0, L, (8, 1, T)), 1)[:, 0] + rng.integers(0, 2, (8, T))
    th = np.where(rng.random((8, T)) < 0.5, at, rng.integers(0, 18, (8, T)))
    return pack(x, hits, pm, th)
def setup_inputs_counts(rng):
    x, hits, pm, th = parts(rng)
    w = np.take_along_axis(pm, rng.integers(0, C, (8, L, 1, H)), 2)[:, :, 0]
    hits = np.stack([x[g][:, w[g]] for g in range(8)])
    o = rng.permutation(8); share = np.zeros((8, 1)); share[o[:5], 0] = np.array([1.0, 0.0, 0.2, 0.5, 0.8])
    th = np.where(rng.random((8, T)) < share, 4081, 0)
    for g in o[5:7]: x[g], hits[g], pm[g] = fall(rng)
    th[o[5]] = 4081; th[o[6]] = np.where(np.arange(T) // V == rng.integers(0, N), 4081, 0)
    x[o[7]], hits[o[7]], pm[o[7]], th[o[7]] = late(rng)
    return pack(x, hits, pm, th)
def setup_inputs_ends(rng):
    x, hits, pm, th = parts(rng)
    x = 255 * rng.integers(0, 2, (8, 16, T)); hits = 255 * rng.integers(0, 2, (8, 16, L, H)); th = rng.choice(np.array([0, 1, 1800, 2040, 2041, 2295, 4080, 4081]), (8, T))
    p = np.ascontiguousarray(pm.reshape(8, L, T)); a, z = np.arange(C), T - 1 - np.arange(C)
    for g in range(8):
        for l, h, want in ((0, 0, z), (L - 1, H - 1, a)):
            for c in range(C):
                k = int(np.nonzero(p[g, l] == want[c])[0][0]); m = c * H + h; was = int(p[g, l, m])
                p[g, l, m] = int(want[c]); p[g, l, k] = was if k != m else int(want[c])
    x[:, :, z] = 0; hits[:, :, 0, 0] = 255; x[:, :, a] = 255; hits[:, :, L - 1, H - 1] = 0
    for t in (z, a): th[:, t] = (np.arange(8) & 1)[:, None]
    p = p.reshape(8, L, C, H); o = rng.permutation(8)
    for g in o[:2]: x[g], hits[g], p[g], th[g] = far(rng)
    x[o[1]] = 255 - x[o[1]]; hits[o[1]] = 255 - hits[o[1]]
    g = int(o[2]); hits[g] = 0; x[g] = 255 - (rng.random((16, T)) < 0.08).astype(np.int64)
    x[g, rng.integers(0, 16, T // 8), rng.permutation(T)[:T // 8]] = 0
    th[g] = rng.choice(np.array([0, 1, 2, 3, 255, 256]), T)
    return pack(x, hits, p, th)
def setup_inputs_alike(rng):
    x, hits, pm, th = parts(rng); pm = np.ascontiguousarray(pm)
    pm[0] = np.arange(T).reshape(C, H); pm[1] = (np.arange(T).reshape(H, C)[:, ::-1]).T; pm[3] = pm[3, 0]; pm[4] = np.arange(T)[::-1].reshape(C, H)
    for g in (0, 4, 6): x[g] = np.tile(x[g][:, :V], (1, N))
    for g in (0, 5): th[g] = rng.integers(0, 2, T)
    x[5] = x[5][:, rng.integers(0, 4, T)]; hits[7] = hits[7][:, :, :1]
    return pack(x, hits, pm, th)
def setup_inputs_spread(rng):
    x, hits, pm, th = parts(rng)
    x = (np.exp2(8 * rng.random((8, 1, T))) * rng.random((8, 16, T))).astype(np.int64)
    hits = (np.exp2(8 * rng.random((8, 1, L, H))) * rng.random((8, 16, L, H))).astype(np.int64)
    th = np.minimum(np.exp2(12 * rng.random((8, T))).astype(np.int64) - 1, 4081)
    return pack(x, hits, pm, th)
def claims(hl, cl):
    a = np.stack([gentries(q) for q in hl]).astype(np.int64).reshape(N, 8, L, V).transpose(1, 2, 0, 3).reshape(8, L, T)
    b = np.stack([gentries(q) for q in cl]).astype(np.int64).reshape(N, 8, C, LN, H).transpose(1, 0, 3, 2, 4).reshape(8, L, C, H)
    return a, b
def check_inputs(d):
    bad = []
    for k in ("fx", "hv"):
        v = d[k].astype(np.float32)
        if not np.all((v >= 0) & (v <= 255) & (v == np.floor(v))): bad.append("whole numbers of " + k)
    for k, hi in (("hl", H - 1), ("cl", T - 1), ("th", 4081)):
        if np.min(d[k]) < 0 or np.max(d[k]) > hi: bad.append("range of " + k)
    if not bad:
        a, b = claims(d["hl"], d["cl"]); b = b.reshape(8, L, T)
        if not np.all(np.sort(b, axis=-1) == np.arange(T)) or not np.all(np.take_along_axis(a, b, 2) == np.tile(np.arange(H), C)): bad.append("claimants of the hits")
    return bad
def reference(fx, hv, hl, cl, th):
    x = fx.astype(np.float32).astype(np.int64).reshape(N, 8, 16, V).transpose(1, 2, 0, 3).reshape(8, 16, T)
    hits = hv.astype(np.float32).astype(np.int64).reshape(N, 8, 16, LN * H).transpose(1, 2, 0, 3).reshape(8, 16, L, H)
    mine, pm = claims(hl, cl); t = th.astype(np.int64).transpose(1, 0, 2).reshape(8, 1, T)
    live = np.ones((8, L, T), bool)
    for rnd in range(RO):
        b = contest(x, hits, live, pm); who, e = apart(x, b, mine)
        live = live & ((who == np.arange(T)) | (e >= t))
        n = np.add.reduce(live.astype(np.int64), axis=1)
        live = live & (n >= MIN)[:, None, :]; n = np.where(n >= MIN, n, 0)
        tot = (L - n)[:, None, :] * x
        for l in range(L): tot = tot + live[:, l][:, None, :] * np.take_along_axis(hits[:, :, l], mine[:, l][:, None, :], 2)
        x = tot >> SH
    return {"yx": np.ascontiguousarray(x.reshape(8, 16, N, V).transpose(2, 0, 1, 3)).reshape(N, 128, V).astype(np.float32).astype(BF),
            "yl": np.ascontiguousarray(live.reshape(8, L, N, V).transpose(2, 0, 1, 3)).reshape(N, 8, L * V).astype(np.float32).astype(BF)}

from concourse.bass import DstId, RemoteDMATransfer
from concourse.mybir import AluOpType as ALU, ActivationFunctionType as ACT

F32, BF, I32, U16 = "float32", "bfloat16", "int32", "uint16"
SCRATCH = {
    "stF": ("dram", [8, 128, 64], BF), "laF": ("dram", [8, 128, 64], BF),
    "stA": ("dram", [8, 128, 128], BF), "laA": ("dram", [8, 128, 128], BF),
    "stB": ("dram", [8, 128, 128], BF), "laB": ("dram", [8, 128, 128], BF),
    "stC": ("dram", [8, 128, 64], I32), "laC": ("dram", [8, 128, 64], I32),
    "stL": ("dram", [8, 128, 64], I32),
    "stX": ("dram", [8, 128, 64], BF), "laX": ("dram", [8, 128, 64], BF),
    "stY": ("dram", [8, 128, 64], BF), "laY": ("dram", [8, 128, 64], BF),
    "xA": ("sbuf", [128, 512], BF), "xB": ("sbuf", [128, 512], BF), "Mk": ("sbuf", [128, 8192], BF),
    "H": ("sbuf", [128, 2064], BF), "Hn": ("sbuf", [128, 2064], BF),
    "clI": ("sbuf", [128, 4, 128], I32), "clF": ("sbuf", [128, 512], F32), "LL": ("sbuf", [128, 8, 64], I32),
    "thA": ("sbuf", [128, 32], I32), "R0": ("sbuf", [128, 128], F32), "R1": ("sbuf", [128, 128], F32),
    "sT": ("sbuf", [128, 256], F32), "TH": ("sbuf", [128, 256], F32),
    "X0": ("sbuf", [128, 4096], F32), "X1": ("sbuf", [128, 4096], F32), "Xb": ("sbuf", [128, 2048], F32),
    "D": ("sbuf", [128, 16384], BF), "Nn": ("sbuf", [128, 16384], BF), "U": ("sbuf", [128, 8192], BF),
    "offA": ("sbuf", [128, 512], U16), "offB": ("sbuf", [128, 128], U16),
    "offC": ("sbuf", [128, 512], U16), "offU": ("sbuf", [128, 512], U16),
    "hlf": ("sbuf", [128, 4, 128], F32), "mx": ("sbuf", [128, 512], F32), "DB": ("sbuf", [128, 4, 128], F32),
    "k2": ("sbuf", [128, 256], F32), "k3": ("sbuf", [128, 256], F32),
    "k4": ("sbuf", [128, 128], I32), "k5": ("sbuf", [128, 128], I32),
    "lu": ("sbuf", [128, 4, 128], F32), "lost": ("sbuf", [128, 4, 128], BF),
    "yy": ("sbuf", [128, 512], F32), "Z": ("sbuf", [128, 512], F32), "tt": ("sbuf", [128, 512], F32),
    "oX": ("sbuf", [128, 512], BF), "oY": ("sbuf", [128, 512], BF),
    "pI": ("sbuf", [128, 8], I32), "pJ": ("sbuf", [128, 16], I32), "col": ("sbuf", [128, 32], F32),
    "ioC": ("sbuf", [128, 256], F32), "io16": ("sbuf", [128, 128], F32), "eq": ("sbuf", [128, 8], F32),
    "Wb": ("sbuf", [128, 144], BF), "Sel": ("sbuf", [128, 512], BF), "Sm": ("sbuf", [128, 240], BF),
    "Sy": ("sbuf", [128, 256], BF), "Pat": ("sbuf", [128, 128], BF), "Wn": ("sbuf", [128, 128], BF),
    "Wo": ("sbuf", [128, 128], BF), "Ip": ("sbuf", [128, 128], BF), "Im": ("sbuf", [128, 128], BF),
    "Ib": ("sbuf", [128, 128], BF), "If": ("sbuf", [128, 128], F32), "Cm": ("sbuf", [128, 128], BF),
    "one": ("sbuf", [128, 512], BF), "Fm": ("sbuf", [128, 128], F32), "Mp": ("sbuf", [128, 128], BF),
    "Mm": ("sbuf", [128, 128], BF),
}
for _b in range(8):
    SCRATCH["P%d" % _b] = ("psum", [128, 512], F32)

_DMAS = ["sF", "oF", "sA", "oA", "sB", "oB", "sC", "oC", "sL", "oL", "lT", "rF", "rG", "rA", "rB", "rC",
         "sX", "oX", "sY", "oY", "wX", "wY"]
_ARR = ["F", "A", "B", "L", "T", "X", "Y"]
SEMAPHORES = ["cV", "cS", "cP", "cG", "sent"] + ["d" + n for n in _DMAS] + ["a" + n for n in _ARR]

MAGIC = 1.5 * 2.0 ** 23
FIXED = ("P0", "P1", "P6", "P7")
CFG = {
    "G": 1.56, "PE": 0.55, "wake": 80.0,
    "A": [["VV", "VV", "VS", "SS", "VV", "SS", "SS", "VS"], ["VV", "VV", "VS", "VS", "VS", "VV", "SS", "SS"]],
    "C": [["VS", "VS", "VS", "VS", "VS", "VS", "VS", "VS"], ["VS", "VS", "VS", "VV", "VS", "VS", "VS", "VS"]],
    "B": [["SS", "SS"], ["SS", "SS"]], "U": ["HVSSSVHV", "SSSHHVVS"], "X": ["VSVSVSVS", "VVVVVVSS", "VSSSSSSS"],
    "J": [[[0, 1], [2, 3]], [[0], [1, 2], [3]]],
    "O": "0a2 0a11 0g2 0g0 0f 0k0 0a0 0g4 0g8 0a1 0a7 0a10 0g12 0a14 0a13 0g3 0l30 0g1 0b0 0l00 0a6 0a4 0g9 0g13 0e 0a15 "
         "0a3 0g10 0u20 0l01 0l21 0a5 0b1 0m05 0z1 0a8 0l11 0u10 0m10 0u21 0g7 0l31 0u01 0g6 0g5 0u31 0o 0m01 0u00 0u11 "
         "0k1 0h 0z3 0m07 0x01 0a12 0x02 0g14 0x13 0g15 0m03 0a9 0u30 0x17 0m02 0x07 0m06 0l20 0x00 0x05 0d1 0x04 1l11 "
         "1g1 0m04 0l10 0x03 0g11 0z0 0m14 0z2 1g3 1a1 1g0 1k0 0x12 0w 0m17 0d0 1g9 0d2 1a2 1a13 0d3 1l01 1g7 1a4 0m15 "
         "1g12 1z0 0m11 1z1 0x16 0x06 0x11 0m00 1g2 1a0 0m13 0x15 1g4 0m12 1g5 1g10 1a3 1a10 1a8 0x10 1z2 1u11 1a5 1l00 "
         "1g6 0x14 1g14 0m16 1b0 1g13 1l31 1b1 1a6 1a12 1u01 1a11 1a7 1a9 1k1 1e 1u30 1g8 1l20 1g11 1l21 1u31 1a15 1u00 "
         "1y 1g15 1u10 1l10 1a14 1u21 1u20 1l30 1z3 1w",
}


def build(g, core, T, topo, cfg):
    me = T.rank_of(core)
    cores = list(T.cores)
    G, PE = cfg["G"], cfg["PE"]
    tasks = []
    lab = [None]

    def task(eng, cost, rd, wr, fn, sem=None, inc=1, lat=0.0, ac=None):
        tasks.append({"eng": eng, "cost": cost, "rd": rd, "wr": wr, "fn": fn, "sem": sem, "inc": inc, "lat": lat, "ac": ac, "lab": lab[0]})
        return tasks[-1]

    def V(n, rd, wr, fn): return task("V", 60 + max(n, 64), rd, wr, fn)
    def S(n, rd, wr, fn): return task("S", 80 + max(n, 64), rd, wr, fn)
    def r(name, lo=0, hi=1 << 20): return (name, lo, hi)
    def A(x): return x[0]() if isinstance(x, list) else x

    def mm(out, lst, rd, wr, n, mul=1):
        def fn():
            ins = None
            for j, (l, x) in enumerate(lst):
                ins = g.tensor.matmul(A(out), l, x, j == 0, j == len(lst) - 1)
            return ins
        return task("P", 40 + len(lst) * max(64, n) * PE * mul, rd, wr, fn)

    def dma(q, name, pairs, rd, wr, lat=2600.0):
        def fn():
            e = g.sync if q == "Y" else g.scalar
            for o, i in pairs:
                e.dma_start(o, i).then_inc(T.sem["d" + name], 16)
            return None
        task(q, 100 * len(pairs), rd, wr, fn, "d" + name, 16 * len(pairs), lat)

    others = [k for k in range(8) if k != me]
    far = [k for k in others if topo.die(cores[k]) != topo.die(core)]
    near = [k for k in others if topo.die(cores[k]) == topo.die(core)]
    lanes = {}
    for j, k in enumerate(far):
        lanes[k] = topo.engines(core, cores[k])[0::2][2 * j:2 * j + 2]
    for j, k in enumerate(near):
        lanes[k] = topo.engines(core, cores[k])[1::2][2 * j:2 * j + 2]
    sent = [0]

    def send(name, parts, rd, wr, lat):
        def fn():
            tr = []
            for k in others:
                rid, pid = topo.addr(cores[k])[:2]
                for j, f in enumerate(parts):
                    es = lanes[k] if len(parts) == 1 else [lanes[k][j]]
                    s, d = f(k)
                    tr.append(RemoteDMATransfer(dst_ids=[DstId(rid=rid, pnc=pid)], dma_engine_mask=sum(1 << e for e in es),
                                                remote_sem=T.sem["a" + name], src=s, dst=d))
            g.remote_dma_fused(tr, local_sem=T.sem.sent)
            return None
        sent[0] += 14
        task("G", 700, rd, wr, fn, "a" + name, 14, lat)

    mine = slice(16 * me, 16 * me + 16)
    dma("Y", "sF", [(T.stF[:], T.fx[:])], [], [r("stF")])
    dma("S", "sC", [(T.stC[:], T.cl[:])], [], [r("stC")], 3000.0)
    dma("Y", "sA", [(T.stA[:], T.hv[:, 0:1024])], [], [r("stA")], 3400.0)
    dma("S", "lT", [(T.thA[:], T.th[:])], [], [r("thA")])
    dma("Y", "oF", [(T.laF[me], T.fx[mine, :])], [], [r("laF.")])
    dma("Y", "oC", [(T.laC[me], T.cl[mine, :])], [], [r("laC.")])
    dma("Y", "oA", [(T.laA[me], T.hv[mine, 0:1024])], [], [r("laA.")])
    dma("S", "sB", [(T.stB[:], T.hv[:, 1024:2048])], [r("stF")], [r("stB")], 3600.0)
    dma("S", "sL", [(T.stL[:, p::16, :], T.hl[p::16, :]) for p in range(16)], [r("stF")], [r("stL")], 3000.0)
    dma("Y", "oB", [(T.laB[me], T.hv[mine, 1024:2048])], [], [r("laB.")])

    def iota(out, name, pat, cm, n, flag):
        def fn():
            if flag:
                return g.iota(out, pat, 0, cm, allow_small_or_imprecise_dtypes=True)
            return g.iota(out, pat, 0, cm)
        task("G", 160 + 2 * n, [], [r(name)], fn)
    iota(T.pI[:, 0:1], "pI", [[1, 1]], 1, 1, False)
    iota(T.io16[:], "io16", [[0, 8], [1, 16]], 0, 128, True)
    iota(T.ioC[:], "ioC", [[1, 256]], 0, 256, True)

    send("F", [lambda k: (T.stF[k], T.laF[me])], [r("stF")], [r("laF")], 6000.0)
    send("A", [lambda k: (T.stC[k], T.laC[me]), lambda k: (T.stA[k], T.laA[me])], [r("stC"), r("stA")], [r("laC"), r("laA")], 7500.0)
    dma("Y", "rF", [(T.xA[0:64, :], T.laF[0:4])], [r("laF"), r("laF.")], [r("xA")])
    dma("Y", "rG", [(T.xB[64:128, :], T.laF[4:8])], [r("laF"), r("laF.")], [r("xB")])
    dma("Y", "rC", [(T.clI[:], T.laC[:])], [r("laC"), r("laC.")], [r("clI")])
    dma("Y", "rA", [(T.H[:, 0:1024], T.laA[:])], [r("laA"), r("laA.")], [r("H", 0, 1024)], 3000.0)
    send("B", [lambda k: (T.stB[k], T.laB[me])], [r("stB"), r("laF")], [r("laB")], 5000.0)
    send("L", [lambda k: (T.stL[k], T.LL[:, me, :])], [r("stL"), r("laA")], [r("LL")], 6500.0)
    dma("Y", "oL", [(T.LL[:, me, :], T.stL[me])], [r("stL")], [r("LL.")])
    dma("Y", "rB", [(T.H[:, 1024:2048], T.laB[:])], [r("laB"), r("laB.")], [r("H", 1024, 2048)])

    v = g.vector
    c = lambda j: T.col[:, j:j + 1]
    rc = lambda j: r("col", j, j + 1)
    PF, PM, PQ, CW, CS, CY, E0, M0, M2, M3, TA, TB, CZ, P3 = range(14)

    def ts(out, in0, s1, s2, op0, op1, n, rd, wr):
        if s2 is None:
            return V(n, rd, wr, lambda: v.tensor_scalar(A(out), A(in0), s1, None, op0))
        return V(n, rd, wr, lambda: v.tensor_scalar(A(out), A(in0), s1, s2, op0, op1))

    def tt(out, in0, in1, op, n, rd, wr):
        return V(n, rd, wr, lambda: v.tensor_tensor(out, A(in0), in1, op))

    def cp(out, in_, n, rd, wr):
        return V(n, rd, wr, lambda: v.tensor_copy(out, A(in_)))

    def ms(ap, val, n, wr):
        return V(n, [], wr, lambda: v.memset(ap, val))

    def act(out, in_, f, n, rd, wr, bias=0.0, scale=1.0):
        return S(n, rd, wr, lambda: g.scalar.activation(out, A(in_), f, bias=bias, scale=scale))

    ts(T.pJ[:, 0:1], T.pI[:, 0:1], 15, None, ALU.bitwise_and, None, 1, [r("pI")], [r("pJ", 0, 1)])
    ts(T.pJ[:, 4:5], T.pI[:, 0:1], 4, None, ALU.arith_shift_right, None, 1, [r("pI")], [r("pJ", 4, 5)])
    ts(T.pJ[:, 8:9], T.pI[:, 0:1], 4, 3, ALU.arith_shift_right, ALU.bitwise_and, 1, [r("pI")], [r("pJ", 8, 9)])
    cp(c(PF), T.pI[:, 0:1], 1, [r("pI")], [rc(PF)])
    cp(c(PM), T.pJ[:, 0:1], 1, [r("pJ", 0, 1)], [rc(PM)])
    cp(c(PQ), T.pJ[:, 4:5], 1, [r("pJ", 4, 5)], [rc(PQ)])
    cp(c(P3), T.pJ[:, 8:9], 1, [r("pJ", 8, 9)], [rc(P3)])
    ts(T.Pat[:], T.io16[:], c(PM), None, ALU.is_equal, None, 128, [r("io16"), rc(PM)], [r("Pat")])
    ts(T.eq[:], T.io16[:, 0:8], c(P3), None, ALU.is_equal, None, 8, [r("io16"), rc(P3)], [r("eq")])
    ts(c(E0), c(PM), 0.0, None, ALU.is_equal, None, 1, [rc(PM)], [rc(E0)])
    ts(c(TA), c(PM), 2.0, 2.0 ** -8, ALU.is_equal, ALU.mult, 1, [rc(PM)], [rc(TA)])
    ts(c(TB), c(PM), 1.0, 2.0 ** -5, ALU.is_equal, ALU.mult, 1, [rc(PM)], [rc(TB)])
    ts(c(CW), c(PQ), 16.0, 15.0, ALU.mult, ALU.add, 1, [rc(PQ)], [rc(CW)])
    for k in range(4):
        ts(T.Sel[:, 128 * k:128 * k + 128], T.Pat[:], T.eq[:, k:k + 1], None, ALU.mult, None, 64,
           [r("Pat"), r("eq")], [r("Sel", 128 * k, 128 * k + 128)])
    ts(c(M0), c(E0), 2.0 ** -12, None, ALU.mult, None, 1, [rc(E0)], [rc(M0)])
    ts(c(M2), c(TA), c(PQ), None, ALU.mult, None, 1, [rc(TA), rc(PQ)], [rc(M2)])
    ts(T.Wb[:], T.ioC[:, 0:144], c(CW), 4096.0, ALU.is_equal, ALU.mult, 144, [r("ioC"), rc(CW)], [r("Wb")])
    ts(c(M3), c(M2), c(TB), None, ALU.add, None, 1, [rc(M2), rc(TB)], [rc(M3)])
    ts(T.Ip[:], T.ioC[:, 0:128], c(PF), None, ALU.is_equal, None, 128, [r("ioC"), rc(PF)], [r("Ip")])
    ts(T.Im[:], T.ioC[:, 0:128], c(PF), -1.0, ALU.is_equal, ALU.mult, 128, [r("ioC"), rc(PF)], [r("Im")])
    for buf, name, part in ((T.xA, "bA", slice(64, 128)), (T.xB, "bB", slice(0, 64))):
        for h, cm in enumerate((M2, M3)):
            ts(buf[part, 256 * h:256 * h + 256], T.ioC[part, :], T.col[part, M0:M0 + 1], T.col[part, cm:cm + 1], ALU.mult, ALU.add, 256,
               [r("ioC"), rc(M0), rc(cm)], [r(name, 256 * h, 256 * h + 256)])
    ts(T.If[:], T.ioC[:, 0:128], c(PF), None, ALU.is_equal, None, 128, [r("ioC"), rc(PF)], [r("If")])

    for b, R in enumerate((T.R0, T.R1)):
        cp(R[:, 0:16], T.thA[:, 16 * b:16 * b + 16], 16, [r("thA")], [r("R%d" % b, 0, 16)])
    for w in (16, 32, 64):
        for b, R in enumerate((T.R0, T.R1)):
            n = "R%d" % b
            cp(R[:, w:2 * w], R[:, 0:w], w, [r(n, 0, w)], [r(n, w, 2 * w)])
    for b, R in enumerate((T.R0, T.R1)):
        P = T["P%d" % (6 + b)]
        mm(P[:, 0:128], [(R[:], T.If[:])], [r("R%d" % b), r("If")], [r("P%d" % (6 + b))], 128, 4)
        act(T.sT[:, b::2], P[:, 0:128], ACT.Copy, 128, [r("P%d" % (6 + b))], [r("sT")], -1024.0, 2048.0)
    send("T", [lambda k: (T.sT[:, 32 * k:32 * k + 32], T.TH[:, 32 * me:32 * me + 32])], [r("sT")], [r("TH")], 4000.0)
    act(T.TH[:, 32 * me:32 * me + 32], T.sT[:, 32 * me:32 * me + 32], ACT.Copy, 32, [r("sT")], [r("TH.")])

    ts(c(CS), c(PM), 112.0, None, ALU.add, None, 1, [rc(PM)], [rc(CS)])
    ts(c(CY), c(PQ), 2.0, 114.0, ALU.mult, ALU.add, 1, [rc(PQ)], [rc(CY)])
    ts(T.Wn[:], T.Pat[:], 2048.0, None, ALU.mult, None, 64, [r("Pat")], [r("Wn")])
    ts(T.Ib[:], T.Ip[:], 32768.0, None, ALU.mult, None, 64, [r("Ip")], [r("Ib")])
    ts(c(CZ), c(CY), c(E0), -1.0, ALU.mult, ALU.add, 1, [rc(CY), rc(E0)], [rc(CZ)])
    ts(T.Sm[:], T.ioC[:, 0:240], c(CS), 1.0 / 16, ALU.is_equal, ALU.mult, 240, [r("ioC"), rc(CS)], [r("Sm")])
    tt(T.Wo[:], T.Wn[:], T.Ib[:], ALU.add, 256, [r("Wn"), r("Ib")], [r("Wo")])
    ts(T.Sy[:], T.ioC[:], c(CZ), 2.0 ** -18, ALU.is_equal, ALU.mult, 256, [r("ioC"), rc(CZ)], [r("Sy")])
    ms(T.Cm[:], -15.0 / 4096, 64, [r("Cm")])
    ms(T.one[:], 1.0, 256, [r("one")])
    ms(T.Mp[:], MAGIC * 32, 64, [r("Mp")])
    ms(T.Mm[:], -MAGIC * 32, 64, [r("Mm")])
    ts(T.Fm[:], T.ioC[:, 0:128], c(PF), -1.0, ALU.is_equal, ALU.mult, 128, [r("ioC"), rc(PF)], [r("Fm")])
    ms(T.H[:, 2048:2064], 2.0 ** 18, 16, [r("H", 2048, 2064)])
    ms(T.Hn[:, 2048:2064], 16128.0, 16, [r("Hn", 2048, 2064)])

    turns = []

    def bank():
        u = {"b": None, "name": "Q%d" % len(turns)}
        turns.append(u)
        return [lambda: T["P%d" % u["b"]][:]], u["name"]

    def spread(k, more=None):
        P, pn = bank()
        x, rd = (T.xA, [r("xA"), r("bA")]) if k < 4 else (T.xB, [r("xB"), r("bB")])
        a = 128 * (k % 4)
        lst, rd = [(T.Sel[:, a:a + 128], x[:])], rd + [r("Sel", a, a + 128)]
        if more is not None:
            lst, rd = [(T.Ip[:], more[0])] + lst, rd + [more[1], r("Ip")]
        mm(P, lst, rd, [r(pn)], 512)
        return P, pn

    def evac(who, o, P, rd, wr):
        if who == "V":
            cp(o, P, 512, rd, wr)
        else:
            act(o, P, ACT.Copy, 512, rd, wr)

    for k in range(8):
        P, pn = spread(k)
        evac(cfg["X"][0][k], T.X0[:, 512 * k:512 * k + 512], P, [r(pn)], [r("X0", 512 * k, 512 * k + 512)])
    for m in range(2):
        cp(T.offA[:, 256 * m:256 * m + 256], T.clI[:, :, 64 * m:64 * m + 64], 256, [r("clI")], [r("offA", 256 * m, 256 * m + 256)])
    lab[0] = "0f"
    for m in range(2):
        cp(T.clF[:, 256 * m:256 * m + 256], T.clI[:, :, 64 * m:64 * m + 64], 256, [r("clI")], [r("clF", 256 * m, 256 * m + 256)])
    lab[0] = "0o"
    for m in range(2):
        a = 256 * m
        cp(T.offC[:, a:a + 256], T.LL[:, :, 32 * m:32 * m + 32], 256, [r("LL"), r("LL.")], [r("offC", a, a + 256)])
        for b in range(2):
            ts(T.hlf[:, :, 64 * m + 32 * b:64 * m + 32 * b + 32], T.LL[:, b::2, 32 * m:32 * m + 32], 18432.0 + 1024 * m, None,
               ALU.add, None, 128, [r("LL"), r("LL.")], [r("hlf", 2 * m + b, 2 * m + b + 1)])
    lab[0] = "0h"
    for h in range(2):
        a = 1024 * h
        act(T.Hn[:, a:a + 1024], T.H[:, a:a + 1024], ACT.Copy, 1024, [r("H", a, a + 1024)], [r("Hn", a, a + 1024)], -256.0)

    def distance(kind, slot, win, wname, off, oname, o0, sub, sname, s0, m, part):
        d0 = 1024 * slot
        D, Nn = T.D[:, d0:d0 + 1024], T.Nn[:, d0:d0 + 1024]
        rD, rN = r("D", d0, d0 + 1024), r("Nn", d0, d0 + 1024)
        ind = win.indirect(off[:, o0:o0 + 64])
        rin = [wname, r(oname, o0, o0 + 64)]
        rs = r(sname, s0, s0 + 1024)
        srcs = [(T.Nn, rN)]
        lab[0] = lab[0][0] + "g%d" % slot
        if kind[0] == "V":
            tt(D, ind, sub[:, s0:s0 + 1024], ALU.subtract, 1024 * G, rin + [rs], [rD])
            lab[0] = lab[0][0] + "a%d" % slot
            if kind[1] == "V":
                ts(Nn, D, 0.0, -2.0, ALU.min, ALU.mult, 512, [rD], [rN])
                srcs = [(T.D, rD), (T.Nn, rN)]
            else:
                act(Nn, D, ACT.Abs, 1024, [rD], [rN])
        else:
            act(D, ind, ACT.Copy, 1024 * G, rin, [rD])
            lab[0] = lab[0][0] + "a%d" % slot
            for h in range(2):
                P, pn = bank()
                a = 512 * h
                mm(P, [(T.Im[:], sub[:, s0 + a:s0 + a + 512]), (T.Ip[:], T.D[:, d0 + a:d0 + a + 512])],
                   [r("Im"), r("Ip"), rs, rD], [r(pn)], 512)
                act(T.Nn[:, d0 + a:d0 + a + 512], P, ACT.Abs, 512, [r(pn)], [r("Nn", d0 + a, d0 + a + 512)])
        lst = [(T.Wb[:, 15 - p:143 - p], buf[:, d0 + p:d0 + 1024:16]) for buf, _ in srcs for p in range(16)]
        rd = [r("Wb")] + [x for _, x in srcs]
        if slot < 8:
            lst = [(T.Mp[:], T.one[:, 0:64])] + lst + [(T.Mm[:], T.one[:, 0:64]), (T.If[:], T.clF[:, o0:o0 + 64])]
            rd = rd + [r("Mp"), r("Mm"), r("one"), r("If"), r("clF", o0, o0 + 64)]
        else:
            lst = [(T.Fm[:], T.TH[:, 64 * part:64 * part + 64])] + lst
            rd = rd + [r("Fm"), r("TH"), r("TH.")]
        mm(T["P%d" % m][:, 64 * part:64 * part + 64], lst, rd, [r("P%d" % m, 64 * part, 64 * part + 64)], 64)["cost"] += 3 * 64 * PE

    def gather(who, out, ind, n, rd, wr):
        if who == "V":
            cp(out, ind, n * G, rd, wr)
        else:
            act(out, ind, ACT.Copy, n * G, rd, wr)

    def acc(P, pn, key, lst, rd):
        t = {}

        def fn():
            ins = None
            for i, (l, x) in enumerate(lst):
                ins = g.tensor.matmul(P[:], l, x, t["t"]["first"] and i == 0, t["t"]["last"] and i == len(lst) - 1)
            return ins
        t["t"] = task("P", 40 + len(lst) * 512 * PE, rd, [r(pn)], fn, None, 1, 0.0, key)

    for rnd in range(2):
        lab[0] = "%d" % rnd
        Xw = [(T.X0, "X0"), (T.X0, "X0") if rnd == 0 else (T.X1, "X1")]
        for m in range(2):
            X, xname = Xw[m]
            for u in range(4):
                distance(cfg["A"][rnd][4 * m + u], 4 * m + u, X[:, 0:4096], r(xname), T.offA, "offA", 256 * m + 64 * u,
                         T.H, "H", 1024 * m, m, u)
            P, pn = T["P%d" % m], "P%d" % m
            b2, b4 = 128 * m, 64 * m
            lab[0] = "%dk%d" % (rnd, m)
            cp(T.k2[:, b2:b2 + 128], P[:, 128:256], 128, [r(pn, 128, 256)], [r("k2", b2, b2 + 128)])
            tt(T.k3[:, b2:b2 + 128], P[:, 0:128], T.k2[:, b2:b2 + 128], ALU.min, 128, [r(pn, 0, 128), r("k2", b2, b2 + 128)], [r("k3", b2, b2 + 128)])
            tt(T.k4[:, b4:b4 + 64], T.k3[:, b2:b2 + 64], T.k3[:, b2 + 64:b2 + 128], ALU.min, 128, [r("k3", b2, b2 + 128)], [r("k4", b4, b4 + 64)])
            ts(T.k5[:, b4:b4 + 64], T.k4[:, b4:b4 + 64], 4095, None, ALU.bitwise_and, None, 64, [r("k4", b4, b4 + 64)], [r("k5", b4, b4 + 64)])
            cp(T.offB[:, b4:b4 + 64], T.k5[:, b4:b4 + 64], 64, [r("k5", b4, b4 + 64)], [r("offB", b4, b4 + 64)])
            lab[0] = "%db%d" % (rnd, m)
            for h in range(2):
                o0, x0 = b4 + 32 * h, 1024 * m + 512 * h
                gather(cfg["B"][rnd][m][h], T.Xb[:, x0:x0 + 512], X[:, 0:4096].indirect(T.offB[:, o0:o0 + 32]), 512,
                       [r(xname), r("offB", o0, o0 + 32)], [r("Xb", x0, x0 + 512)])

        lab[0] = "%dw" % rnd
        mark = 2.0 ** 14 if rnd == 0 else 2.0 ** 18
        act(T.yy[0:64, :], T.xA[0:64, :], ACT.Copy, 512, [r("xA")], [r("yy", 0, 1)], 1.0, -1.0 / mark)
        act(T.yy[64:128, :], T.xB[64:128, :], ACT.Copy, 512, [r("xB")], [r("yy", 1, 2)], 1.0, -1.0 / mark)
        Hw, hn = (T.Hn, "Hn") if rnd == 0 else (T.H, "H")
        acc(T.P7, "P7", ("x", rnd), [(T.Cm[:], T.one[:])], [r("Cm"), r("one")])
        late = []
        for js in cfg["J"][rnd]:
            j0, j1 = js[0], js[-1] + 1
            w = 64 * (j1 - j0)
            for m in range(2):
                X, xname = Xw[m]
                for u in js:
                    distance(cfg["C"][rnd][4 * m + u], 8 + 4 * m + u, T.Xb[:, 1024 * m:1024 * m + 1024], r("Xb", 1024 * m, 1024 * m + 1024),
                             T.offC, "offC", 256 * m + 64 * u, X, xname, 1024 * u, m, u)
                P, pn = T["P%d" % m], "P%d" % m
                a = 64 * j0
                rp, rq = r(pn, a, a + w), r(pn, 256 + a, 256 + a + w)
                lo, rl = T.lost[:, j0:j1, 64 * m:64 * m + 64], r("lost%d" % m, j0, j1)
                lab[0] = "%dl%d%d" % (rnd, j0, m)
                act(P[:, 256 + a:256 + a + w], P[:, a:a + w], ACT.Abs, w, [rp], [rq])
                if rnd == 0:
                    tt(lo, P[:, 256 + a:256 + a + w], T.TH[:, a:a + w], ALU.is_lt, w, [rq, r("TH"), r("TH.")], [rl])
                else:
                    tt(lo, P[:, 256 + a:256 + a + w], T.DB[:, j0:j1, 64 * m:64 * m + 64], ALU.is_lt, w, [rq, r("DB%d" % m, j0, j1)], [rl])
            lab[0] = "%dz%d" % (rnd, j0)
            for u in js:
                for m in range(2):
                    a = 128 * u + 64 * m
                    mm(T.P6[:, a:a + 64], [(T.Wn[:], T.lost[:, u, 64 - 64 * m:128 - 64 * m]), (T.Wo[:], T.lost[:, u, 64 * m:64 * m + 64])],
                       [r("Wn"), r("Wo"), r("lost0", u, u + 1), r("lost1", u, u + 1)], [r("P6", a, a + 64)], 64)
            a, w = 128 * j0, 2 * w
            tt(T.mx[:, a:a + w], T.P6[:, a:a + w], T.hlf[:, j0:j1, :], ALU.max, w, [r("P6", a, a + w), r("hlf")], [r("mx", a, a + w)])
            ts(T.offU[:, a:a + w], T.mx[:, a:a + w], -18432.0, 2048.0, ALU.add, ALU.min, w, [r("mx", a, a + w)], [r("offU", a, a + w)])
            if rnd == 0:
                lab[0] = "0d%d" % j0
                act(T.lu[:, j0:j1, :], T.mx[:, a:a + w], ACT.Copy, w, [r("mx", a, a + w)], [r("lu", j0, j1)], -20479.5e10, 1e10)
                for m in range(2):
                    tt(T.DB[:, j0:j1, 64 * m:64 * m + 64], T.lu[:, j0:j1, 64 * m:64 * m + 64], T.TH[:, 64 * j0:64 * j1], ALU.max, w,
                       [r("lu", j0, j1), r("TH"), r("TH.")], [r("DB%d" % m, j0, j1)])
            for u in js:
                for m in range(2):
                    lab[0] = "%du%d%d" % (rnd, u, m)
                    o0, u0 = 128 * u + 64 * m, 4096 * m + 1024 * u
                    who = cfg["U"][rnd][2 * u + m]
                    if who == "H":
                        for h, e in enumerate("VS"):
                            gather(e, T.U[:, u0 + 512 * h:u0 + 512 * h + 512], Hw[:, 0:2064].indirect(T.offU[:, o0 + 32 * h:o0 + 32 * h + 32]), 512,
                                   [r(hn), r("offU", o0, o0 + 64)], [r("U", u0 + 512 * h, u0 + 512 * h + 512)])
                    else:
                        gather(who, T.U[:, u0:u0 + 1024], Hw[:, 0:2064].indirect(T.offU[:, o0:o0 + 64]), 1024,
                               [r(hn), r("offU", o0, o0 + 64)], [r("U", u0, u0 + 1024)])
                    for k in (2 * u, 2 * u + 1):
                        x, rx = T.U[:, 4096 * m + 512 * k:4096 * m + 512 * k + 512], r("U", 4096 * m + 512 * k, 4096 * m + 512 * k + 512)
                        acc(T.P7, "P7", ("x", rnd), [(T.Sm[:, 112 - 16 * k:240 - 16 * k], x)], [rx, r("Sm")])
                        if rnd == 1:
                            late.append(([(T.Sy[:, 113 - 16 * k - m:241 - 16 * k - m], x)], [rx, r("Sy")]))
        lab[0] = "%dy" % rnd
        for lst, rd in late:
            acc(T.P0, "P0", ("y", rnd), lst, rd)
        lab[0] = "%de" % rnd
        big = MAGIC * mark / 16
        ts(T.P1[:], T.P7[:], big, big, ALU.add, ALU.subtract, 512, [r("P7")], [r("P1")])
        tt(T.Z[:], T.P1[:], T.yy[:], ALU.mult, 512, [r("P1"), r("yy")], [r("Z")])
        tt(T.tt[:], T.P7[:], T.Z[:], ALU.subtract, 512, [r("P7"), r("Z")], [r("tt")])
        if rnd == 0:
            ts(T.xA[0:64, :], T.tt[0:64, :], MAGIC + 256, MAGIC, ALU.add, ALU.subtract, 512, [r("tt")], [r("xA")])
            ts(T.xB[64:128, :], T.tt[64:128, :], MAGIC + 256, MAGIC, ALU.add, ALU.subtract, 512, [r("tt")], [r("xB")])
            for m in range(2):
                X, xname = (T.X0, "X0") if m == 0 else (T.X1, "X1")
                for k in range(8):
                    lab[0] = "0x%d%d" % (m, k)
                    a = 4096 * m + 512 * k
                    o, w = X[:, 512 * k:512 * k + 512], [r(xname, 512 * k, 512 * k + 512)]
                    if cfg["X"][1 + m][k] == "V":
                        P, pn = spread(k)
                        tt(o, P, T.U[:, a:a + 512], ALU.max, 512, [r(pn), r("U", a, a + 512)], w)
                    else:
                        mk, rm = T.Mk[:, a:a + 512], r("Mk", a, a + 512)
                        lab[0] = "0m%d%d" % (m, k)
                        act(mk, T.U[:, a:a + 512], ACT.Relu, 512, [r("U", a, a + 512)], [rm])
                        lab[0] = "0x%d%d" % (m, k)
                        P, pn = spread(k, (mk, rm))
                        evac("S", o, P, [r(pn)], w)
        else:
            act(T.oY[:], T.P0[:], ACT.Copy, 512, [r("P0")], [r("oY")], 1.0, -1.0)
            ts(T.oX[:], T.tt[:], MAGIC, MAGIC, ALU.add, ALU.subtract, 512, [r("tt")], [r("oX")])

    dma("S", "sY", [(T.stY[:], T.oY[:])], [r("oY")], [r("stY")])
    dma("S", "oY", [(T.laY[me], T.oY[mine, :])], [r("oY")], [r("laY.")])
    dma("Y", "sX", [(T.stX[:], T.oX[:])], [r("oX")], [r("stX")])
    dma("Y", "oX", [(T.laX[me], T.oX[mine, :])], [r("oX")], [r("laX.")])
    send("Y", [lambda k: (T.stY[k], T.laY[me])], [r("stY")], [r("laY")], 3000.0)
    send("X", [lambda k: (T.stX[k], T.laX[me])], [r("stX")], [r("laX")], 3000.0)
    dma("S", "wY", [(T.yl[:], T.laY[:])], [r("laY"), r("laY.")], [r("yl")])
    dma("Y", "wX", [(T.yx[:], T.laX[:])], [r("laX"), r("laX.")], [r("yx")])
    return tasks, turns, sent[0]


def depends(tasks):
    hist = {}
    line = {}
    for i, t in enumerate(tasks):
        dep = set()
        acc = [(x, False) for x in t["rd"]] + [(x, True) for x in t["wr"]]
        for (name, lo, hi), w in acc:
            for (j, l2, h2, w2) in hist.get(name, []):
                if l2 < hi and lo < h2 and (w or w2) and not (t["ac"] is not None and tasks[j]["ac"] == t["ac"]):
                    dep.add(j)
        for (name, lo, hi), w in acc:
            if w and t["ac"] is None:
                hist[name] = [e for e in hist.get(name, []) if not (lo <= e[1] and e[2] <= hi)]
            hist.setdefault(name, []).append((i, lo, hi, w))
        dep.discard(i)
        t["dep"] = dep
        t["banks"] = sorted(set(x[0] for x, _ in acc if x[0] in FIXED))
        t["after"] = line.get(t["eng"])
        if t["eng"] in "GY":
            line[t["eng"]] = i


def arrange(tasks, cfg):
    n, wake = len(tasks), cfg["wake"]
    succ = [[] for _ in range(n)]
    wait = [0] * n
    for i, t in enumerate(tasks):
        pre = set(t["dep"])
        if t["after"] is not None:
            pre.add(t["after"])
        wait[i] = len(pre)
        for j in pre:
            succ[j].append(i)
    place0 = {k: j for j, k in enumerate(cfg["O"].split())}
    rank = [-i if t["lab"] is None else -1000 * (1 + place0.get(t["lab"], 999)) - i for i, t in enumerate(tasks)]
    busy = {}
    ready = [i for i in range(n) if wait[i] == 0]
    end = 0.0
    place = {}
    while ready:
        i = max(ready, key=lambda k: rank[k])
        ready.remove(i)
        place[i] = len(place)
        t = tasks[i]
        st = max([tasks[j]["end"] + (wake if tasks[j]["eng"] != "P" or t["eng"] != "P" else 0.0) for j in t["dep"]] + [0.0])
        if t["after"] is not None:
            st = max(st, tasks[t["after"]]["at"] + tasks[t["after"]]["cost"])
        taken = list(busy.get(t["eng"], []))
        for b in t["banks"]:
            taken += [(a - wake, z + wake) for a, z, e in busy.get(b, []) if e != t["eng"]]
        for iv in sorted(taken):
            if iv[1] > st and iv[0] < st + t["cost"]:
                st = iv[1]
        t["at"], t["end"] = st, st + t["cost"] + t["lat"]
        end = max(end, t["end"])
        busy.setdefault(t["eng"], []).append((st, st + t["cost"]))
        for b in t["banks"]:
            busy.setdefault(b, []).append((st, st + t["cost"], t["eng"]))
        for j in succ[i]:
            wait[j] -= 1
            if wait[j] == 0:
                ready.append(j)
    return sorted(range(n), key=lambda k: (tasks[k]["at"], place[k])), end


def plan(tasks, turns, cfg):
    depends(tasks)
    order, end = arrange(tasks, cfg)
    writer, reader = {}, {}
    for i, t in enumerate(tasks):
        for x in t["wr"]:
            writer[x[0]] = i
        for x in t["rd"]:
            reader[x[0]] = i
    turns = sorted(turns, key=lambda u: (tasks[reader[u["name"]]]["at"], reader[u["name"]]))
    for k, u in enumerate(turns):
        u["b"] = 2 + k % 4
        if k >= 4:
            tasks[writer[u["name"]]]["dep"].add(reader[turns[k - 4]["name"]])
    order, end = arrange(tasks, cfg)
    last, sums = {}, {}
    for i in order:
        t = tasks[i]
        for b in t["banks"]:
            for e, j in last.setdefault(b, {}).items():
                if e != t["eng"]:
                    t["dep"].add(j)
            last[b][t["eng"]] = i
        if t["ac"] is not None:
            sums.setdefault(t["ac"], []).append(i)
    for lst in sums.values():
        for k, i in enumerate(lst):
            tasks[i]["first"], tasks[i]["last"] = k == 0, k == len(lst) - 1
    return order, end


def rank_program(g, core, T, topo):
    if T.rank_of(core) is None:
        return
    tasks, turns, sent = build(g, core, T, topo, CFG)
    order, _ = plan(tasks, turns, CFG)
    queue = {"V": g.vector, "S": g.scalar, "P": g.tensor, "G": g, "Y": g.sync}
    count = {"V": 0, "S": 0, "P": 0, "G": 0}
    waited = {}
    total = {}
    for i in order:
        t = tasks[i]
        e = t["eng"]
        need = {}
        for j in t["dep"]:
            d = tasks[j]
            if e == "P" and d["eng"] == "P":
                continue
            s, val = d["sig"]
            need[s] = max(need.get(s, 0), val)
        for s in sorted(need):
            if waited.get((e, s), 0) < need[s]:
                queue[e].wait_ge(T.sem[s], need[s])
                waited[(e, s)] = need[s]
        ins = t["fn"]()
        if t["sem"] is None:
            count[e] += 1
            ins.then_inc(T.sem["c" + e], 1)
            t["sig"] = ("c" + e, count[e])
        else:
            t["sig"] = (t["sem"], t["inc"])
        total[t["sig"][0]] = t["sig"][1]
    total["sent"] = sent
    seen = {}
    for (e, s), val in waited.items():
        seen[s] = max(seen.get(s, 0), val)
    for s in sorted(total):
        if seen.get(s, 0) < total[s]:
            g.sync.wait_ge(T.sem[s], total[s])
